import numpy as np
import ml_dtypes


def mxq(x, axis, fmt="e4m3"):
    dtype, down = {"e4m3": (ml_dtypes.float8_e4m3fn, 7), "e5m2": (ml_dtypes.float8_e5m2, 14)}[fmt]
    v = np.moveaxis(np.asarray(x, np.float32).astype(ml_dtypes.bfloat16).astype(np.float64), axis, -1)
    blocks = v.reshape(v.shape[:-1] + (-1, 32))
    amax = np.abs(blocks).max(-1, keepdims=True)
    byte = np.maximum(np.where(amax > 0, np.frexp(amax)[1] - 1 + 127, 0) - down, 1)
    scale = np.exp2(byte - 127.0)
    codes = (blocks / scale).astype(np.float32).astype(dtype).astype(np.float64)
    return np.moveaxis((codes * scale).reshape(v.shape), -1, axis)


WIDE = False


def mx_kscale(k, group=512):
    if not WIDE:
        return np.ones(k)
    levels = np.array([18, -18])
    if group != 512:
        return np.exp2(np.random.permutation(np.resize(levels, k // group))).repeat(group)
    if k % 512:
        return np.exp2(np.random.permutation(np.resize(levels, k // 32))).repeat(32)
    a = np.empty((k // 512, 16))
    for p in range(k // 512):
        a[p, :8] = np.random.permutation(np.resize(levels, 8))
        for g in range(8):
            far = levels[np.abs(levels - a[p, g]) >= 10]
            a[p, g + 8] = far[np.random.randint(len(far))]
    return np.exp2(a.ravel()).repeat(32)


def f64(x):
    return np.asarray(x).astype(np.float64)


def sigmoid(v):
    return 1.0 / (1.0 + np.exp(-v))


def bf(x):
    return np.asarray(x, np.float32).astype(ml_dtypes.bfloat16)


def planes(Y):
    r, m = Y.shape
    b = f64(bf(Y)).reshape(r // 32, 32, m)
    amax = np.abs(b).max(1)
    byte = np.clip(np.where(amax > 0, np.frexp(amax)[1] - 1 + 127 - 7, 1), 1, 254)
    codes = (b * np.exp2(127.0 - byte)[:, None, :]).reshape(r, m).astype(np.float32).astype(ml_dtypes.float8_e4m3fn).view(np.uint8)
    words = codes.reshape(r // 512, 128, 4, m).transpose(0, 1, 3, 2)
    return np.ascontiguousarray(words), np.ascontiguousarray(byte.astype(np.uint8).reshape(r // 512, 16, m))


G, D, M, N = 4, 128, 128, 512


def setup_inputs():
    n = np.random.standard_normal
    s_d = mx_kscale(D, 0)
    return {
        "h": (n((G, D, N)) * s_d[:, None]).astype(np.float32),
        "wf": (n((G, D, M)) / np.sqrt(D) / s_d[:, None]).astype(np.float32),
        "xf": (n((G, M, N))).astype(np.float32),
        "xc": (n((G, M, N))).astype(np.float32),
        "hp": (n((G, M, N))).astype(np.float32),
    }


def reference(h, wf, xf, xc, hp):
    wfq = mxq(f64(wf), 1, "e4m3")
    hq = mxq(f64(h), 1, "e4m3")
    zf = wfq.transpose(0, 2, 1) @ hq
    f = sigmoid(zf + f64(xf))
    y = f * np.tanh(f64(xc)) + (1.0 - f) * f64(hp)
    Y = y.reshape(G * M, N)
    words, scales = planes(Y)
    return Y, words, scales

@@ -1,0 +1,170 @@
+from contextlib import ExitStack
+
+import concourse.mybir as mybir
+
+G, D, M, N = 4, 128, 128, 512
+FLOPS = 2 * G * D * M * N
+
+F32 = mybir.dt.float32
+BF16 = mybir.dt.bfloat16
+I32 = mybir.dt.int32
+U32 = mybir.dt.uint32
+U8 = mybir.dt.uint8
+FP8X4 = mybir.dt.float8_e4m3fn_x4
+ALU = mybir.AluOpType
+ACT = mybir.ActivationFunctionType
+
+P = 128
+PACK = 4
+ROWS = 32
+CH = 128
+NCH = N // CH
+H_PIECES = ((0, 256), (256, 128), (384, 128))
+
+
+def interleave(copy, dst, src):
+    copy(out=dst.rearrange("p (c i) t -> p c t i", i=4), in_=src.rearrange("p t (c i) -> p c t i", i=4))
+
+
+def tile_rows_pl_cell_mgu_kernel(tc, h, wf, xf, xc, hp, out_0, out_1, out_2):
+    nc = tc.nc
+    h_rows = h.rearrange("g (p j) n -> (g p) j n", j=PACK)
+    w_rows = wf.rearrange("g (p j) m -> (g p) j m", j=PACK)
+    words_hbm = out_1.rearrange("s p n u -> (s p) (n u)").bitcast(I32)
+    scales_hbm = out_2.rearrange("s b n -> (s b) n").bitcast(I32).rearrange("(g b) (c n) -> c b g n", g=G, c=NCH)
+
+    with ExitStack() as ctx:
+        sb = ctx.enter_context(tc.tile_pool(name="sb", bufs=1))
+        ps = ctx.enter_context(tc.psum_pool(name="ps", bufs=1))
+        ctx.enter_context(tc.manual_schedule())
+
+        def tiles(name, shape, dtype):
+            return [sb.tile(shape, dtype, name="%s%d" % (name, g), align_bytes=64) for g in range(G)]
+
+        w_raw = sb.tile([P, PACK, M], F32, name="w_raw")
+        w_bf = sb.tile([P, M, PACK], BF16, name="w_bf", align_bytes=64)
+        w_codes = sb.tile([P, M], U32, name="w_codes", align_bytes=64)
+        w_scales = sb.tile([P, M], U8, name="w_scales", align_bytes=64)
+        h_raw = [sb.tile([P, PACK, w], F32, name="h_raw%d" % i) for i, (s, w) in enumerate(H_PIECES)]
+        h_bf = [sb.tile([P, w, PACK], BF16, name="h_bf%d" % i, align_bytes=64) for i, (s, w) in enumerate(H_PIECES)]
+        h_codes = sb.tile([P, N], U32, name="h_codes", align_bytes=64)
+        h_scales = sb.tile([P, N], U8, name="h_scales", align_bytes=64)
+        xf_sb = tiles("xf", [P, N], F32)
+        xc_sb = tiles("xc", [P, N], F32)
+        hp_sb = tiles("hp", [P, N], F32)
+        pre = tiles("pre", [P, N], F32)
+        gate = tiles("gate", [P, N], F32)
+        cand = tiles("cand", [P, N], F32)
+        diff = tiles("diff", [P, N], F32)
+        prod = tiles("prod", [P, N], F32)
+        y = tiles("y", [P, N], F32)
+        y_rows = tiles("y_rows", [P, PACK, CH], F32)
+        y_bf = tiles("y_bf", [P, CH, PACK], BF16)
+        y_codes = [sb.tile([P, 2, CH], U32, name="y_codes%d" % i, align_bytes=64) for i in range(G // 2)]
+        y_scales = sb.tile([P, G, CH], U8, name="y_scales", align_bytes=64)
+        z = [ps.tile([P, N], F32, name="z%d" % g) for g in range(G)]
+
+        nc.sync.dma_start(out=w_raw[:], in_=w_rows)
+        for i, (s, w) in enumerate(H_PIECES):
+            nc.sync.dma_start(out=h_raw[i][:], in_=h_rows[:, :, s : s + w])
+        for g in range(G):
+            nc.sync.dma_start(out=xf_sb[g][:], in_=xf[g])
+            nc.sync.dma_start(out=xc_sb[g][:], in_=xc[g])
+            nc.sync.dma_start(out=hp_sb[g][:], in_=hp[g])
+
+        def quantize(codes, scales, src):
+            nc.vector.quantize_mx(out=codes.bitcast(FP8X4), scales=scales, in_=src.rearrange("p w j -> p (w j)"))
+
+        def quantize_h(i):
+            s, w = H_PIECES[i]
+            quantize(h_codes[:, s : s + w], h_scales[:, s : s + w], h_bf[i][:])
+
+        def products(groups, chunks):
+            for g, c in [(g, c) for g in groups for c in chunks]:
+                cols = slice(c * CH, (c + 1) * CH)
+                rows = slice(g * ROWS, (g + 1) * ROWS)
+                nc.tensor.matmul_mx(
+                    out=z[g][:, cols],
+                    lhsT=w_codes[rows, :].bitcast(FP8X4),
+                    lhsT_scale=w_scales[rows, :],
+                    rhs=h_codes[rows, cols].bitcast(FP8X4),
+                    rhs_scale=h_scales[rows, cols],
+                    start=True,
+                    stop=True,
+                )
+
+        interleave(nc.vector.tensor_copy, w_bf[:], w_raw[:])
+        quantize(w_codes[:], w_scales[:], w_bf[:])
+        interleave(nc.vector.tensor_copy, h_bf[0][:], h_raw[0][:])
+        interleave(nc.scalar.copy, h_bf[1][:], h_raw[1][:])
+        quantize_h(0)
+        products((0, 1), (0, 1))
+        interleave(nc.vector.tensor_copy, h_bf[2][:], h_raw[2][:])
+        quantize_h(1)
+        products((0, 1), (2,))
+        quantize_h(2)
+        products((0, 1), (3,))
+        products((2, 3), range(NCH))
+
+        def add_pre(g):
+            nc.vector.tensor_tensor(out=pre[g][:], in0=z[g][:], in1=xf_sb[g][:], op=ALU.add)
+            nc.scalar.activation(out=gate[g][:], in_=pre[g][:], func=ACT.Tanh, scale=0.5)
+
+        def tanh_cand(g):
+            nc.scalar.activation(out=cand[g][:], in_=xc_sb[g][:], func=ACT.Tanh)
+
+        def sub_diff(g):
+            nc.vector.tensor_tensor(out=diff[g][:], in0=cand[g][:], in1=hp_sb[g][:], op=ALU.subtract)
+
+        def mul_prod(g):
+            nc.vector.scalar_tensor_tensor(
+                out=prod[g][:], in0=gate[g][:], scalar=1.0, in1=diff[g][:], op0=ALU.add, op1=ALU.mult
+            )
+
+        def mix(g):
+            nc.vector.scalar_tensor_tensor(
+                out=y[g][:], in0=prod[g][:], scalar=0.5, in1=hp_sb[g][:], op0=ALU.mult, op1=ALU.add
+            )
+            for c in range(NCH):
+                queue = nc.scalar if (g == G - 1 and c >= 2) else nc.sync
+                queue.dma_start(out=y_rows[g][c * ROWS : (c + 1) * ROWS, :, :], in_=y[g][:, c * CH : (c + 1) * CH])
+            nc.sync.dma_start(out=out_0[g * M : (g + 1) * M, :], in_=y[g][:])
+
+        def round_y(g):
+            interleave(nc.scalar.copy, y_bf[g][:], y_rows[g][:])
+
+        def quantize_y(g):
+            quantize(y_codes[g // 2][:, g % 2, :], y_scales[:, g, :], y_bf[g][:])
+
+        def store_words(pair, queues):
+            dst = words_hbm[2 * pair * ROWS : 2 * (pair + 1) * ROWS, :].rearrange("(g q) (c n) -> c q g n", g=2, c=NCH)
+            for c in range(NCH):
+                queues[c].dma_start(out=dst[c], in_=y_codes[pair][c * ROWS : (c + 1) * ROWS, :, :].bitcast(I32))
+
+        tanh_cand(0)
+        add_pre(0)
+        sub_diff(0)
+        for g in range(G - 1):
+            tanh_cand(g + 1)
+            add_pre(g + 1)
+            mul_prod(g)
+            sub_diff(g + 1)
+            mix(g)
+        last = G - 1
+        round_y(0)
+        round_y(1)
+        mul_prod(last)
+        quantize_y(0)
+        mix(last)
+        round_y(2)
+        quantize_y(1)
+        store_words(0, [nc.sync] * NCH)
+        quantize_y(2)
+        split = 80
+        interleave(nc.vector.tensor_copy, y_bf[last][:, :split, :], y_rows[last][:, :, :split])
+        interleave(nc.scalar.copy, y_bf[last][:, split:, :], y_rows[last][:, :, split:])
+        quantize_y(last)
+        queues = [nc.sync, nc.scalar, nc.sync, nc.scalar]
+        store_words(1, queues)
+        for c in range(NCH):
+            queues[c].dma_start(out=scales_hbm[c], in_=y_scales[c * ROWS : c * ROWS + 4, :, :].bitcast(I32))

@@ -19,7 +19,9 @@ PACK = 4
 ROWS = 32
 CH = 128
 NCH = N // CH
+H_LOADS = ((0, 256), (256, 256))
 H_PIECES = ((0, 256), (256, 128), (384, 128))
+HALF = N // 2
 
 
 def interleave(copy, dst, src):
@@ -31,7 +33,7 @@ def tile_rows_pl_cell_mgu_kernel(tc, h, wf, xf, xc, hp, out_0, out_1, out_2):
     h_rows = h.rearrange("g (p j) n -> (g p) j n", j=PACK)
     w_rows = wf.rearrange("g (p j) m -> (g p) j m", j=PACK)
     words_hbm = out_1.rearrange("s p n u -> (s p) (n u)").bitcast(I32)
-    scales_hbm = out_2.rearrange("s b n -> (s b) n").bitcast(I32).rearrange("(g b) (c n) -> c b g n", g=G, c=NCH)
+    scales_hbm = out_2.rearrange("s b n -> (s b) n").bitcast(I32).rearrange("(s g b) (c n) -> c g b s n", s=2, g=2, c=2)
 
     with ExitStack() as ctx:
         sb = ctx.enter_context(tc.tile_pool(name="sb", bufs=1))
@@ -45,7 +47,7 @@ def tile_rows_pl_cell_mgu_kernel(tc, h, wf, xf, xc, hp, out_0, out_1, out_2):
         w_bf = sb.tile([P, M, PACK], BF16, name="w_bf", align_bytes=64)
         w_codes = sb.tile([P, M], U32, name="w_codes", align_bytes=64)
         w_scales = sb.tile([P, M], U8, name="w_scales", align_bytes=64)
-        h_raw = [sb.tile([P, PACK, w], F32, name="h_raw%d" % i) for i, (s, w) in enumerate(H_PIECES)]
+        h_raw = [sb.tile([P, PACK, w], F32, name="h_raw%d" % i) for i, (s, w) in enumerate(H_LOADS)]
         h_bf = [sb.tile([P, w, PACK], BF16, name="h_bf%d" % i, align_bytes=64) for i, (s, w) in enumerate(H_PIECES)]
         h_codes = sb.tile([P, N], U32, name="h_codes", align_bytes=64)
         h_scales = sb.tile([P, N], U8, name="h_scales", align_bytes=64)
@@ -58,14 +60,15 @@ def tile_rows_pl_cell_mgu_kernel(tc, h, wf, xf, xc, hp, out_0, out_1, out_2):
         diff = tiles("diff", [P, N], F32)
         prod = tiles("prod", [P, N], F32)
         y = tiles("y", [P, N], F32)
-        y_rows = tiles("y_rows", [P, PACK, CH], F32)
-        y_bf = tiles("y_bf", [P, CH, PACK], BF16)
-        y_codes = [sb.tile([P, 2, CH], U32, name="y_codes%d" % i, align_bytes=64) for i in range(G // 2)]
-        y_scales = sb.tile([P, G, CH], U8, name="y_scales", align_bytes=64)
+        y_bf = tiles("y_bf", [P, N], BF16)
+        y_rows = [sb.tile([P, PACK, HALF], BF16, name="y_rows%d" % i, align_bytes=64) for i in range(2)]
+        y_pack = [sb.tile([P, HALF, PACK], BF16, name="y_pack%d" % i, align_bytes=64) for i in range(2)]
+        y_codes = [sb.tile([P, HALF], U32, name="y_codes%d" % i, align_bytes=64) for i in range(2)]
+        y_scales = sb.tile([P, 2, HALF], U8, name="y_scales", align_bytes=64)
         z = [ps.tile([P, N], F32, name="z%d" % g) for g in range(G)]
 
         nc.sync.dma_start(out=w_raw[:], in_=w_rows)
-        for i, (s, w) in enumerate(H_PIECES):
+        for i, (s, w) in enumerate(H_LOADS):
             nc.sync.dma_start(out=h_raw[i][:], in_=h_rows[:, :, s : s + w])
         for g in range(G):
             nc.sync.dma_start(out=xf_sb[g][:], in_=xf[g])
@@ -96,14 +99,17 @@ def tile_rows_pl_cell_mgu_kernel(tc, h, wf, xf, xc, hp, out_0, out_1, out_2):
         interleave(nc.vector.tensor_copy, w_bf[:], w_raw[:])
         quantize(w_codes[:], w_scales[:], w_bf[:])
         interleave(nc.vector.tensor_copy, h_bf[0][:], h_raw[0][:])
-        interleave(nc.scalar.copy, h_bf[1][:], h_raw[1][:])
         quantize_h(0)
         products((0, 1), (0, 1))
-        interleave(nc.vector.tensor_copy, h_bf[2][:], h_raw[2][:])
+        hs = 48
+        interleave(nc.vector.tensor_copy, h_bf[1][:], h_raw[1][:, :, :CH])
+        interleave(nc.vector.tensor_copy, h_bf[2][:, :hs, :], h_raw[1][:, :, CH : CH + hs])
+        interleave(nc.scalar.copy, h_bf[2][:, hs:, :], h_raw[1][:, :, CH + hs :])
         quantize_h(1)
-        products((0, 1), (2,))
+        products((0,), (2,))
         quantize_h(2)
-        products((0, 1), (3,))
+        products((0,), (3,))
+        products((1,), (2, 3))
         products((2, 3), range(NCH))
 
         def add_pre(g):
@@ -116,55 +122,74 @@ def tile_rows_pl_cell_mgu_kernel(tc, h, wf, xf, xc, hp, out_0, out_1, out_2):
         def sub_diff(g):
             nc.vector.tensor_tensor(out=diff[g][:], in0=cand[g][:], in1=hp_sb[g][:], op=ALU.subtract)
 
-        def mul_prod(g):
+        def mul_prod(g, cols=slice(0, N)):
             nc.vector.scalar_tensor_tensor(
-                out=prod[g][:], in0=gate[g][:], scalar=1.0, in1=diff[g][:], op0=ALU.add, op1=ALU.mult
+                out=prod[g][:, cols], in0=gate[g][:, cols], scalar=1.0, in1=diff[g][:, cols], op0=ALU.add, op1=ALU.mult
             )
 
-        def mix(g):
+        def mix(g, dst, cols=slice(0, N)):
             nc.vector.scalar_tensor_tensor(
-                out=y[g][:], in0=prod[g][:], scalar=0.5, in1=hp_sb[g][:], op0=ALU.mult, op1=ALU.add
+                out=dst[g][:, cols], in0=prod[g][:, cols], scalar=0.5, in1=hp_sb[g][:, cols], op0=ALU.mult, op1=ALU.add
             )
-            for c in range(NCH):
-                queue = nc.scalar if (g == G - 1 and c >= 2) else nc.sync
-                queue.dma_start(out=y_rows[g][c * ROWS : (c + 1) * ROWS, :, :], in_=y[g][:, c * CH : (c + 1) * CH])
+
+        def regroup(g, halves):
+            for c in halves:
+                first = (2 * c + g % 2) * ROWS
+                nc.sync.dma_start(
+                    out=y_rows[g // 2][first : first + ROWS, :, :], in_=y_bf[g][:, c * HALF : (c + 1) * HALF]
+                )
+
+        def store_y(g):
             nc.sync.dma_start(out=out_0[g * M : (g + 1) * M, :], in_=y[g][:])
 
-        def round_y(g):
-            interleave(nc.scalar.copy, y_bf[g][:], y_rows[g][:])
-
-        def quantize_y(g):
-            quantize(y_codes[g // 2][:, g % 2, :], y_scales[:, g, :], y_bf[g][:])
+        def quantize_y(pair):
+            quantize(y_codes[pair][:], y_scales[:, pair, :], y_pack[pair][:])
 
         def store_words(pair, queues):
-            dst = words_hbm[2 * pair * ROWS : 2 * (pair + 1) * ROWS, :].rearrange("(g q) (c n) -> c q g n", g=2, c=NCH)
-            for c in range(NCH):
-                queues[c].dma_start(out=dst[c], in_=y_codes[pair][c * ROWS : (c + 1) * ROWS, :, :].bitcast(I32))
+            for c in range(2):
+                queues[c].dma_start(
+                    out=words_hbm[64 * pair : 64 * (pair + 1), c * HALF : (c + 1) * HALF],
+                    in_=y_codes[pair][64 * c : 64 * (c + 1), :].bitcast(I32),
+                )
 
+        def round_y(g):
+            nc.scalar.copy(out=y_bf[g][:], in_=y[g][:])
+            regroup(g, (0, 1))
+            store_y(g)
+
+        last = G - 1
         tanh_cand(0)
         add_pre(0)
         sub_diff(0)
-        for g in range(G - 1):
+        for g in range(last):
             tanh_cand(g + 1)
+            if g > 0:
+                round_y(g - 1)
             add_pre(g + 1)
             mul_prod(g)
             sub_diff(g + 1)
-            mix(g)
-        last = G - 1
-        round_y(0)
-        round_y(1)
-        mul_prod(last)
+            if g < last - 1:
+                mix(g, y)
+        mix(last - 1, y_bf)
+        regroup(last - 1, (0, 1))
+        interleave(nc.scalar.copy, y_pack[0][:], y_rows[0][:])
+        for c in range(2):
+            mul_prod(last, slice(c * HALF, (c + 1) * HALF))
+        for c in range(2):
+            mix(last, y_bf, slice(c * HALF, (c + 1) * HALF))
+            regroup(last, (c,))
+        for g in (last - 1, last):
+            mix(g, y)
+            store_y(g)
         quantize_y(0)
-        mix(last)
-        round_y(2)
+        store_words(0, (nc.sync, nc.sync))
+        split = 160
+        interleave(nc.vector.tensor_copy, y_pack[1][:, :split, :], y_rows[1][:, :, :split])
+        interleave(nc.scalar.copy, y_pack[1][:, split:, :], y_rows[1][:, :, split:])
         quantize_y(1)
-        store_words(0, [nc.sync] * NCH)
-        quantize_y(2)
-        split = 80
-        interleave(nc.vector.tensor_copy, y_bf[last][:, :split, :], y_rows[last][:, :, :split])
-        interleave(nc.scalar.copy, y_bf[last][:, split:, :], y_rows[last][:, :, split:])
-        quantize_y(last)
-        queues = [nc.sync, nc.scalar, nc.sync, nc.scalar]
-        store_words(1, queues)
-        for c in range(NCH):
-            queues[c].dma_start(out=scales_hbm[c], in_=y_scales[c * ROWS : c * ROWS + 4, :, :].bitcast(I32))
+        store_words(1, (nc.sync, nc.scalar))
+        for c in range(2):
+            for g in range(2):
+                first = (2 * c + g) * ROWS
+                queue = nc.sync if g == 0 else nc.scalar
+                queue.dma_start(out=scales_hbm[c, g], in_=y_scales[first : first + 4, :, :].bitcast(I32))

@@ -122,28 +122,34 @@ def tile_rows_pl_cell_mgu_kernel(tc, h, wf, xf, xc, hp, out_0, out_1, out_2):
         def sub_diff(g):
             nc.vector.tensor_tensor(out=diff[g][:], in0=cand[g][:], in1=hp_sb[g][:], op=ALU.subtract)
 
-        def mul_prod(g, cols=slice(0, N)):
+        def part(t, piece):
+            if piece is None:
+                return t[:]
+            return t[:].rearrange("p (c j n) -> p j c n", c=2, j=2)[:, piece, :, :]
+
+        def mul_prod(g, piece=None):
             nc.vector.scalar_tensor_tensor(
-                out=prod[g][:, cols], in0=gate[g][:, cols], scalar=1.0, in1=diff[g][:, cols], op0=ALU.add, op1=ALU.mult
+                out=part(prod[g], piece), in0=part(gate[g], piece), scalar=1.0, in1=part(diff[g], piece), op0=ALU.add, op1=ALU.mult
             )
 
-        def mix(g, dst, cols=slice(0, N)):
+        def mix(g, dst, piece=None):
             nc.vector.scalar_tensor_tensor(
-                out=dst[g][:, cols], in0=prod[g][:, cols], scalar=0.5, in1=hp_sb[g][:, cols], op0=ALU.mult, op1=ALU.add
+                out=part(dst[g], piece), in0=part(prod[g], piece), scalar=0.5, in1=part(hp_sb[g], piece), op0=ALU.mult, op1=ALU.add
             )
 
-        def regroup(g, halves):
-            for c in halves:
+        def regroup(g, start=0, width=HALF):
+            for c in range(2):
                 first = (2 * c + g % 2) * ROWS
                 nc.sync.dma_start(
-                    out=y_rows[g // 2][first : first + ROWS, :, :], in_=y_bf[g][:, c * HALF : (c + 1) * HALF]
+                    out=y_rows[g // 2][first : first + ROWS, :, start : start + width],
+                    in_=y_bf[g][:, c * HALF + start : c * HALF + start + width],
                 )
 
         def store_y(g):
             nc.sync.dma_start(out=out_0[g * M : (g + 1) * M, :], in_=y[g][:])
 
-        def quantize_y(pair):
-            quantize(y_codes[pair][:], y_scales[:, pair, :], y_pack[pair][:])
+        def quantize_y(pair, cols=slice(0, HALF)):
+            quantize(y_codes[pair][:, cols], y_scales[:, pair, cols], y_pack[pair][:, cols, :])
 
         def store_words(pair, queues):
             for c in range(2):
@@ -154,7 +160,7 @@ def tile_rows_pl_cell_mgu_kernel(tc, h, wf, xf, xc, hp, out_0, out_1, out_2):
 
         def round_y(g):
             nc.scalar.copy(out=y_bf[g][:], in_=y[g][:])
-            regroup(g, (0, 1))
+            regroup(g)
             store_y(g)
 
         last = G - 1
@@ -171,22 +177,24 @@ def tile_rows_pl_cell_mgu_kernel(tc, h, wf, xf, xc, hp, out_0, out_1, out_2):
             if g < last - 1:
                 mix(g, y)
         mix(last - 1, y_bf)
-        regroup(last - 1, (0, 1))
+        regroup(last - 1)
         interleave(nc.scalar.copy, y_pack[0][:], y_rows[0][:])
         for c in range(2):
-            mul_prod(last, slice(c * HALF, (c + 1) * HALF))
+            mul_prod(last, c)
         for c in range(2):
-            mix(last, y_bf, slice(c * HALF, (c + 1) * HALF))
-            regroup(last, (c,))
+            mix(last, y_bf, c)
+            regroup(last, c * CH, CH)
         for g in (last - 1, last):
             mix(g, y)
             store_y(g)
         quantize_y(0)
         store_words(0, (nc.sync, nc.sync))
-        split = 160
-        interleave(nc.vector.tensor_copy, y_pack[1][:, :split, :], y_rows[1][:, :, :split])
-        interleave(nc.scalar.copy, y_pack[1][:, split:, :], y_rows[1][:, :, split:])
-        quantize_y(1)
+        for start, share in ((0, 64), (CH, 80)):
+            cut, end = start + share, start + CH
+            interleave(nc.vector.tensor_copy, y_pack[1][:, start:cut, :], y_rows[1][:, :, start:cut])
+            interleave(nc.scalar.copy, y_pack[1][:, cut:end, :], y_rows[1][:, :, cut:end])
+        quantize_y(1, slice(0, CH))
+        quantize_y(1, slice(CH, HALF))
         store_words(1, (nc.sync, nc.scalar))
         for c in range(2):
             for g in range(2):

from contextlib import ExitStack

import concourse.mybir as mybir

G, D, M, N = 4, 128, 128, 512
FLOPS = 2 * G * D * M * N

F32 = mybir.dt.float32
BF16 = mybir.dt.bfloat16
I32 = mybir.dt.int32
U32 = mybir.dt.uint32
U8 = mybir.dt.uint8
FP8X4 = mybir.dt.float8_e4m3fn_x4
ALU = mybir.AluOpType
ACT = mybir.ActivationFunctionType

P = 128
PACK = 4
ROWS = 32
CH = 128
NCH = N // CH
H_LOADS = ((0, 256), (256, 256))
H_PIECES = ((0, 256), (256, 128), (384, 128))
HALF = N // 2


def interleave(copy, dst, src):
    copy(out=dst.rearrange("p (c i) t -> p c t i", i=4), in_=src.rearrange("p t (c i) -> p c t i", i=4))


def tile_rows_pl_cell_mgu_kernel(tc, h, wf, xf, xc, hp, out_0, out_1, out_2):
    nc = tc.nc
    h_rows = h.rearrange("g (p j) n -> (g p) j n", j=PACK)
    w_rows = wf.rearrange("g (p j) m -> (g p) j m", j=PACK)
    words_hbm = out_1.rearrange("s p n u -> (s p) (n u)").bitcast(I32)
    scales_hbm = out_2.rearrange("s b n -> (s b) n").bitcast(I32).rearrange("(s g b) (c n) -> c g b s n", s=2, g=2, c=2)

    with ExitStack() as ctx:
        sb = ctx.enter_context(tc.tile_pool(name="sb", bufs=1))
        ps = ctx.enter_context(tc.psum_pool(name="ps", bufs=1))
        ctx.enter_context(tc.manual_schedule())

        def tiles(name, shape, dtype):
            return [sb.tile(shape, dtype, name="%s%d" % (name, g), align_bytes=64) for g in range(G)]

        w_raw = sb.tile([P, PACK, M], F32, name="w_raw")
        w_bf = sb.tile([P, M, PACK], BF16, name="w_bf", align_bytes=64)
        w_codes = sb.tile([P, M], U32, name="w_codes", align_bytes=64)
        w_scales = sb.tile([P, M], U8, name="w_scales", align_bytes=64)
        h_raw = [sb.tile([P, PACK, w], F32, name="h_raw%d" % i) for i, (s, w) in enumerate(H_LOADS)]
        h_bf = [sb.tile([P, w, PACK], BF16, name="h_bf%d" % i, align_bytes=64) for i, (s, w) in enumerate(H_PIECES)]
        h_codes = sb.tile([P, N], U32, name="h_codes", align_bytes=64)
        h_scales = sb.tile([P, N], U8, name="h_scales", align_bytes=64)
        xf_sb = tiles("xf", [P, N], F32)
        xc_sb = tiles("xc", [P, N], F32)
        hp_sb = tiles("hp", [P, N], F32)
        pre = tiles("pre", [P, N], F32)
        gate = tiles("gate", [P, N], F32)
        cand = tiles("cand", [P, N], F32)
        diff = tiles("diff", [P, N], F32)
        prod = tiles("prod", [P, N], F32)
        y = tiles("y", [P, N], F32)
        y_bf = tiles("y_bf", [P, N], BF16)
        y_rows = [sb.tile([P, PACK, HALF], BF16, name="y_rows%d" % i, align_bytes=64) for i in range(2)]
        y_pack = [sb.tile([P, HALF, PACK], BF16, name="y_pack%d" % i, align_bytes=64) for i in range(2)]
        y_codes = [sb.tile([P, HALF], U32, name="y_codes%d" % i, align_bytes=64) for i in range(2)]
        y_scales = sb.tile([P, 2, HALF], U8, name="y_scales", align_bytes=64)
        z = [ps.tile([P, N], F32, name="z%d" % g) for g in range(G)]

        nc.sync.dma_start(out=w_raw[:], in_=w_rows)
        for i, (s, w) in enumerate(H_LOADS):
            nc.sync.dma_start(out=h_raw[i][:], in_=h_rows[:, :, s : s + w])
        for g in range(G):
            nc.sync.dma_start(out=xf_sb[g][:], in_=xf[g])
            nc.sync.dma_start(out=xc_sb[g][:], in_=xc[g])
            nc.sync.dma_start(out=hp_sb[g][:], in_=hp[g])

        def quantize(codes, scales, src):
            nc.vector.quantize_mx(out=codes.bitcast(FP8X4), scales=scales, in_=src.rearrange("p w j -> p (w j)"))

        def quantize_h(i):
            s, w = H_PIECES[i]
            quantize(h_codes[:, s : s + w], h_scales[:, s : s + w], h_bf[i][:])

        def products(groups, chunks):
            for g, c in [(g, c) for g in groups for c in chunks]:
                cols = slice(c * CH, (c + 1) * CH)
                rows = slice(g * ROWS, (g + 1) * ROWS)
                nc.tensor.matmul_mx(
                    out=z[g][:, cols],
                    lhsT=w_codes[rows, :].bitcast(FP8X4),
                    lhsT_scale=w_scales[rows, :],
                    rhs=h_codes[rows, cols].bitcast(FP8X4),
                    rhs_scale=h_scales[rows, cols],
                    start=True,
                    stop=True,
                )

        interleave(nc.vector.tensor_copy, w_bf[:], w_raw[:])
        quantize(w_codes[:], w_scales[:], w_bf[:])
        interleave(nc.vector.tensor_copy, h_bf[0][:], h_raw[0][:])
        quantize_h(0)
        products((0, 1), (0, 1))
        hs = 48
        interleave(nc.vector.tensor_copy, h_bf[1][:], h_raw[1][:, :, :CH])
        interleave(nc.vector.tensor_copy, h_bf[2][:, :hs, :], h_raw[1][:, :, CH : CH + hs])
        interleave(nc.scalar.copy, h_bf[2][:, hs:, :], h_raw[1][:, :, CH + hs :])
        quantize_h(1)
        products((0,), (2,))
        quantize_h(2)
        products((0,), (3,))
        products((1,), (2, 3))
        products((2, 3), range(NCH))

        def add_pre(g):
            nc.vector.tensor_tensor(out=pre[g][:], in0=z[g][:], in1=xf_sb[g][:], op=ALU.add)
            nc.scalar.activation(out=gate[g][:], in_=pre[g][:], func=ACT.Tanh, scale=0.5)

        def tanh_cand(g):
            nc.scalar.activation(out=cand[g][:], in_=xc_sb[g][:], func=ACT.Tanh)

        def sub_diff(g):
            nc.vector.tensor_tensor(out=diff[g][:], in0=cand[g][:], in1=hp_sb[g][:], op=ALU.subtract)

        def part(t, piece):
            if piece is None:
                return t[:]
            return t[:].rearrange("p (c j n) -> p j c n", c=2, j=2)[:, piece, :, :]

        def mul_prod(g, piece=None):
            nc.vector.scalar_tensor_tensor(
                out=part(prod[g], piece), in0=part(gate[g], piece), scalar=1.0, in1=part(diff[g], piece), op0=ALU.add, op1=ALU.mult
            )

        def mix(g, dst, piece=None):
            nc.vector.scalar_tensor_tensor(
                out=part(dst[g], piece), in0=part(prod[g], piece), scalar=0.5, in1=part(hp_sb[g], piece), op0=ALU.mult, op1=ALU.add
            )

        def regroup(g, start=0, width=HALF):
            for c in range(2):
                first = (2 * c + g % 2) * ROWS
                nc.sync.dma_start(
                    out=y_rows[g // 2][first : first + ROWS, :, start : start + width],
                    in_=y_bf[g][:, c * HALF + start : c * HALF + start + width],
                )

        def store_y(g):
            nc.sync.dma_start(out=out_0[g * M : (g + 1) * M, :], in_=y[g][:])

        def quantize_y(pair, cols=slice(0, HALF)):
            quantize(y_codes[pair][:, cols], y_scales[:, pair, cols], y_pack[pair][:, cols, :])

        def store_words(pair, queues):
            for c in range(2):
                queues[c].dma_start(
                    out=words_hbm[64 * pair : 64 * (pair + 1), c * HALF : (c + 1) * HALF],
                    in_=y_codes[pair][64 * c : 64 * (c + 1), :].bitcast(I32),
                )

        def round_y(g):
            nc.scalar.copy(out=y_bf[g][:], in_=y[g][:])
            regroup(g)
            store_y(g)

        last = G - 1
        tanh_cand(0)
        add_pre(0)
        sub_diff(0)
        for g in range(last):
            tanh_cand(g + 1)
            if g > 0:
                round_y(g - 1)
            add_pre(g + 1)
            mul_prod(g)
            sub_diff(g + 1)
            if g < last - 1:
                mix(g, y)
        mix(last - 1, y_bf)
        regroup(last - 1)
        interleave(nc.scalar.copy, y_pack[0][:], y_rows[0][:])
        for c in range(2):
            mul_prod(last, c)
        for c in range(2):
            mix(last, y_bf, c)
            regroup(last, c * CH, CH)
        for g in (last - 1, last):
            mix(g, y)
            store_y(g)
        quantize_y(0)
        store_words(0, (nc.sync, nc.sync))
        for start, share in ((0, 64), (CH, 80)):
            cut, end = start + share, start + CH
            interleave(nc.vector.tensor_copy, y_pack[1][:, start:cut, :], y_rows[1][:, :, start:cut])
            interleave(nc.scalar.copy, y_pack[1][:, cut:end, :], y_rows[1][:, :, cut:end])
        quantize_y(1, slice(0, CH))
        quantize_y(1, slice(CH, HALF))
        store_words(1, (nc.sync, nc.scalar))
        for c in range(2):
            for g in range(2):
                first = (2 * c + g) * ROWS
                queue = nc.sync if g == 0 else nc.scalar
                queue.dma_start(out=scales_hbm[c, g], in_=y_scales[first : first + 4, :, :].bitcast(I32))
